import numpy as np
CORES = [0,9,18,27,36,45,54,63,64,73,82,91,100,109,118,127]
N = 16
def setup_inputs(rng):
    return {"x": rng.standard_normal((N, 128, 256), dtype=np.float32)}
def reference(x):
    g = np.ascontiguousarray(x.transpose(1, 2, 0)).reshape(128, 256 * N)
    return {"y": np.broadcast_to(g, (N,) + g.shape)}

@@ -1,0 +1,155 @@
+from concourse.bass import DstId, RemoteDMATransfer
+
+SCRATCH = {
+    "xs": ("dram", [16, 128, 16], "float32"),
+    "H": ("dram", [2, 128, 16], "float32"),
+    "A": ("sbuf", [128, 32], "float32"),
+    "Y": ("sbuf", [128, 4096], "float32"),
+}
+SEMAPHORES = (["ld", "h", "a0", "a1", "b", "snd", "st"]
+              + ["fw%d" % c for c in range(16)] + ["ry%d" % c for c in range(16)])
+
+CAP = (2, 3, 6, 7)
+NON = (0, 1, 4, 5)
+FWD = {0: 2, 1: 2, 2: 3, 3: 3, 4: 6, 5: 6, 6: 7, 7: 7}
+FIDX = {2: 0, 3: 1, 6: 2, 7: 3}
+
+
+def shares(r):
+    kr = r % 8
+    other = [c for c in range(16) if (c & 1) != (r & 1)]
+    same = [(r + 2 * t) % 16 for t in range(1, 8)]
+    out = {k: [] for k in range(8)}
+    for n, c in enumerate(other):
+        out[CAP[n // 2]].append(c)
+    order = [k for k in NON if k != kr] + ([kr] if kr in NON else [])
+    for n, c in enumerate(same):
+        out[order[n // 2]].append(c)
+    return out
+
+
+def fw_expect(f, b, c):
+    if c != b:
+        return 16
+    return 4 * len([w for w in range(8) if FWD[w] == f and w != f])
+
+
+def rank_program(g, core, T, topo):
+    chip, k = divmod(core, 8)
+    S = T.sem
+    kr = chip % 8
+    is_rank = (k == kr)
+    sent = [0]
+
+    def tr(src, dsts, mask, sem):
+        ids = []
+        for d, _ap in dsts:
+            rid, pid, _se = topo.addr(d)
+            ids.append(DstId(rid=rid, pnc=pid))
+        sent[0] += bin(mask).count("1")
+        return RemoteDMATransfer(dst_ids=ids, dma_engine_mask=mask, remote_sem=sem,
+                                 srcs=[src], dsts=[ap for _d, ap in dsts])
+
+    def fused(trs):
+        g.remote_dma_fused(trs, local_sem=S.snd)
+
+    def a_cols(s):
+        return T.A[:, 16 * s:16 * s + 16]
+
+    sh = shares(chip)
+    slot = chip // 8
+    asem = S["a%d" % slot]
+
+    def exchange(srcs):
+        trs = []
+        for n, c in enumerate(sh[k]):
+            trs.append(tr(srcs[n], [(c * 8 + kr, a_cols(slot))], 0x0F << (4 * n), asem))
+        if trs:
+            fused(trs)
+
+    if is_rank:
+        g.sync.dma_start(T.xs[:], T.x[:]).then_inc(S.ld, 16)
+        g.scalar.dma_start(a_cols(slot), T.x[8 * chip:8 * chip + 8, :]).then_inc(asem, 16)
+        g.wait_ge(S.ld, 16)
+        trs = []
+        for h in range(8):
+            if h == k:
+                continue
+            for n, c in enumerate(sh[h]):
+                trs.append(tr(T.xs[c], [(chip * 8 + h, T.H[n])], 1 << len(trs), S.h))
+        fused(trs)
+        exchange([T.xs[c] for c in sh[k]])
+    else:
+        g.wait_ge(S.h, len(sh[k]))
+        exchange([T.H[n] for n in range(len(sh[k]))])
+
+    order = (slot, 1 - slot) if is_rank else (0, 1)
+    for s in order:
+        r = k + 8 * s
+        sem = S["a%d" % s]
+        need = 16 if r == chip else 4
+        q = g.sync if s == 0 else g.scalar
+        g.wait_ge(sem, need)
+        trs = []
+        for i in range(16):
+            w = i // 2
+            if w == k:
+                continue
+            col = 256 * chip + 32 * w + 16 * (i % 2) + r
+            trs.append(tr(T.A[:, 16 * s + i:16 * s + i + 1], [(chip * 8 + w, T.Y[:, col:col + 1])],
+                          1 << (len(trs) + 2 * s), S.b))
+        fused(trs)
+        q.wait_ge(sem, need)
+        for i in (2 * k, 2 * k + 1):
+            col = 256 * chip + 32 * k + 16 * (i % 2) + r
+            q.dma_start(T.Y[:, col:col + 1], T.A[:, 16 * s + i:16 * s + i + 1]).then_inc(S.b, 16)
+
+    B_ALL = 28 + 64
+    g.wait_ge(S.b, B_ALL)
+    lo = 256 * chip + 32 * k
+    mine = T.Y[:, lo:lo + 32]
+    fk = FWD[k]
+    fsem = S["fw%d" % chip]
+    trs = [tr(mine, [(((chip + 2 * t) % 16) * 8 + fk, mine) for t in range(1, 8)], 0x00FF, fsem)]
+    if fk != k:
+        trs.append(tr(mine, [(chip * 8 + fk, mine)], 0x0F00, fsem))
+    if kr != k and kr != fk:
+        trs.append(tr(mine, [(chip * 8 + kr, mine)], 0xF000, S["ry%d" % chip]))
+    fused(trs)
+
+    if k in CAP:
+        mate = chip ^ 1
+        for t in range(8):
+            c = (chip - 2 * t) % 16
+            need = fw_expect(k, chip, c)
+            if need:
+                g.wait_ge(S["fw%d" % c], need)
+            lo = 256 * c + 64 * FIDX[k]
+            part = T.Y[:, lo:lo + 64]
+            rsem = S["ry%d" % c]
+            trs = [tr(part, [(mate * 8 + mate % 8, part)], 0x00FF, rsem)]
+            if c != chip and not is_rank:
+                trs.append(tr(part, [(chip * 8 + kr, part)], 0xFF00, rsem))
+            fused(trs)
+
+    if is_rank:
+        nfw = len([f for f in CAP if f != k])
+        for t in range(8):
+            c = (chip - 2 * t) % 16
+            q = g.sync
+            if c == chip:
+                q.wait_ge(S.b, B_ALL)
+                q.wait_ge(S["ry%d" % c], 4 * len([w for w in range(8) if w != k and FWD[w] != k]))
+            else:
+                q.wait_ge(S["ry%d" % c], 8 * nfw)
+            if k in CAP and fw_expect(k, chip, c):
+                q.wait_ge(S["fw%d" % c], fw_expect(k, chip, c))
+            q.dma_start(T.y[8 * c:8 * c + 8, :], T.Y[:, 256 * c:256 * c + 256]).then_inc(S.st, 16)
+        for t in range(8):
+            c = ((chip ^ 1) - 2 * t) % 16
+            q = g.scalar
+            q.wait_ge(S["ry%d" % c], 32)
+            q.dma_start(T.y[8 * c:8 * c + 8, :], T.Y[:, 256 * c:256 * c + 256]).then_inc(S.st, 16)
+        g.wait_ge(S.st, 256)
+
+    g.wait_ge(S.snd, sent[0])

@@ -83,26 +83,28 @@ def rank_program(g, core, T, topo):
         g.wait_ge(S.h, len(sh[k]))
         exchange([T.H[n] for n in range(len(sh[k]))])
 
-    order = (slot, 1 - slot) if is_rank else (0, 1)
-    for s in order:
-        r = k + 8 * s
-        sem = S["a%d" % s]
-        need = 16 if r == chip else 4
+    def column(s, i):
+        col = 256 * chip + 16 * i + (k + 8 * s)
+        return T.Y[:, col:col + 1], T.A[:, 16 * s + i:16 * s + i + 1]
+
+    for s in (0, 1):
+        need = 16 if k + 8 * s == chip else 4
         q = g.sync if s == 0 else g.scalar
-        g.wait_ge(sem, need)
+        g.wait_ge(S["a%d" % s], need)
+        q.wait_ge(S["a%d" % s], need)
+        for i in (2 * k, 2 * k + 1):
+            dst, src = column(s, i)
+            q.dma_start(dst, src).then_inc(S.b, 16)
+    for group in (CAP, NON):
         trs = []
-        for i in range(16):
-            w = i // 2
+        for w in group:
             if w == k:
                 continue
-            col = 256 * chip + 32 * w + 16 * (i % 2) + r
-            trs.append(tr(T.A[:, 16 * s + i:16 * s + i + 1], [(chip * 8 + w, T.Y[:, col:col + 1])],
-                          1 << (len(trs) + 2 * s), S.b))
+            for s in (0, 1):
+                for i in (2 * w, 2 * w + 1):
+                    dst, src = column(s, i)
+                    trs.append(tr(src, [(chip * 8 + w, dst)], 1 << len(trs), S.b))
         fused(trs)
-        q.wait_ge(sem, need)
-        for i in (2 * k, 2 * k + 1):
-            col = 256 * chip + 32 * k + 16 * (i % 2) + r
-            q.dma_start(T.Y[:, col:col + 1], T.A[:, 16 * s + i:16 * s + i + 1]).then_inc(S.b, 16)
 
     B_ALL = 28 + 64
     g.wait_ge(S.b, B_ALL)

@@ -12,7 +12,6 @@ SEMAPHORES = (["ld", "h", "a0", "a1", "b", "snd", "st"]
 CAP = (2, 3, 6, 7)
 NON = (0, 1, 4, 5)
 FWD = {0: 2, 1: 2, 2: 3, 3: 3, 4: 6, 5: 6, 6: 7, 7: 7}
-FIDX = {2: 0, 3: 1, 6: 2, 7: 3}
 
 
 def shares(r):
@@ -28,10 +27,9 @@ def shares(r):
     return out
 
 
-def fw_expect(f, b, c):
-    if c != b:
-        return 16
-    return 4 * len([w for w in range(8) if FWD[w] == f and w != f])
+def fwd_core(b, w):
+    f = FWD[w]
+    return f ^ 1 if f == b % 8 else f
 
 
 def rank_program(g, core, T, topo):
@@ -110,47 +108,49 @@ def rank_program(g, core, T, topo):
     g.wait_ge(S.b, B_ALL)
     lo = 256 * chip + 32 * k
     mine = T.Y[:, lo:lo + 32]
-    fk = FWD[k]
+    fk = fwd_core(chip, k)
     fsem = S["fw%d" % chip]
-    trs = [tr(mine, [(((chip + 2 * t) % 16) * 8 + fk, mine) for t in range(1, 8)], 0x00FF, fsem)]
+    dsts = []
+    for t in range(1, 8):
+        b = (chip + 2 * t) % 16
+        dsts.append((b * 8 + fwd_core(b, k), mine))
+    trs = [tr(mine, dsts, 0x00FF, fsem)]
     if fk != k:
         trs.append(tr(mine, [(chip * 8 + fk, mine)], 0x0F00, fsem))
-    if kr != k and kr != fk:
+    if kr != k:
         trs.append(tr(mine, [(chip * 8 + kr, mine)], 0xF000, S["ry%d" % chip]))
     fused(trs)
 
-    if k in CAP:
+    if k in CAP and not is_rank:
         mate = chip ^ 1
+        ws = [w for w in range(8) if fwd_core(chip, w) == k]
         for t in range(8):
             c = (chip - 2 * t) % 16
-            need = fw_expect(k, chip, c)
-            if need:
-                g.wait_ge(S["fw%d" % c], need)
-            lo = 256 * c + 64 * FIDX[k]
-            part = T.Y[:, lo:lo + 64]
+            need = 8 * len(ws) if c != chip else 4 * len([w for w in ws if w != k])
+            g.wait_ge(S["fw%d" % c], need)
+            lo = 256 * c + 32 * min(ws)
+            part = T.Y[:, lo:lo + 32 * len(ws)]
             rsem = S["ry%d" % c]
             trs = [tr(part, [(mate * 8 + mate % 8, part)], 0x00FF, rsem)]
-            if c != chip and not is_rank:
+            if c != chip:
                 trs.append(tr(part, [(chip * 8 + kr, part)], 0xFF00, rsem))
             fused(trs)
 
     if is_rank:
-        nfw = len([f for f in CAP if f != k])
+        nfw = 8 * (3 if k in CAP else 4)
         for t in range(8):
             c = (chip - 2 * t) % 16
             q = g.sync
             if c == chip:
                 q.wait_ge(S.b, B_ALL)
-                q.wait_ge(S["ry%d" % c], 4 * len([w for w in range(8) if w != k and FWD[w] != k]))
+                q.wait_ge(S["ry%d" % c], 28)
             else:
-                q.wait_ge(S["ry%d" % c], 8 * nfw)
-            if k in CAP and fw_expect(k, chip, c):
-                q.wait_ge(S["fw%d" % c], fw_expect(k, chip, c))
+                q.wait_ge(S["ry%d" % c], nfw)
             q.dma_start(T.y[8 * c:8 * c + 8, :], T.Y[:, 256 * c:256 * c + 256]).then_inc(S.st, 16)
         for t in range(8):
             c = ((chip ^ 1) - 2 * t) % 16
             q = g.scalar
-            q.wait_ge(S["ry%d" % c], 32)
+            q.wait_ge(S["ry%d" % c], nfw)
             q.dma_start(T.y[8 * c:8 * c + 8, :], T.Y[:, 256 * c:256 * c + 256]).then_inc(S.st, 16)
         g.wait_ge(S.st, 256)
 

from concourse.bass import DstId, RemoteDMATransfer

SCRATCH = {
    "xs": ("dram", [16, 128, 16], "float32"),
    "H": ("dram", [2, 128, 16], "float32"),
    "A": ("sbuf", [128, 32], "float32"),
    "Y": ("sbuf", [128, 4096], "float32"),
}
SEMAPHORES = (["ld", "h", "a0", "a1", "b", "snd", "st"]
              + ["fw%d" % c for c in range(16)] + ["ry%d" % c for c in range(16)])

CAP = (2, 3, 6, 7)
NON = (0, 1, 4, 5)
FWD = {0: 2, 1: 2, 2: 3, 3: 3, 4: 6, 5: 6, 6: 7, 7: 7}


def shares(r):
    kr = r % 8
    other = [c for c in range(16) if (c & 1) != (r & 1)]
    same = [(r + 2 * t) % 16 for t in range(1, 8)]
    out = {k: [] for k in range(8)}
    for n, c in enumerate(other):
        out[CAP[n // 2]].append(c)
    order = [k for k in NON if k != kr] + ([kr] if kr in NON else [])
    for n, c in enumerate(same):
        out[order[n // 2]].append(c)
    return out


def fwd_core(b, w):
    f = FWD[w]
    return f ^ 1 if f == b % 8 else f


def rank_program(g, core, T, topo):
    chip, k = divmod(core, 8)
    S = T.sem
    kr = chip % 8
    is_rank = (k == kr)
    sent = [0]

    def tr(src, dsts, mask, sem):
        ids = []
        for d, _ap in dsts:
            rid, pid, _se = topo.addr(d)
            ids.append(DstId(rid=rid, pnc=pid))
        sent[0] += bin(mask).count("1")
        return RemoteDMATransfer(dst_ids=ids, dma_engine_mask=mask, remote_sem=sem,
                                 srcs=[src], dsts=[ap for _d, ap in dsts])

    def fused(trs):
        g.remote_dma_fused(trs, local_sem=S.snd)

    def a_cols(s):
        return T.A[:, 16 * s:16 * s + 16]

    sh = shares(chip)
    slot = chip // 8
    asem = S["a%d" % slot]

    def exchange(srcs):
        trs = []
        for n, c in enumerate(sh[k]):
            trs.append(tr(srcs[n], [(c * 8 + kr, a_cols(slot))], 0x0F << (4 * n), asem))
        if trs:
            fused(trs)

    if is_rank:
        g.sync.dma_start(T.xs[:], T.x[:]).then_inc(S.ld, 16)
        g.scalar.dma_start(a_cols(slot), T.x[8 * chip:8 * chip + 8, :]).then_inc(asem, 16)
        g.wait_ge(S.ld, 16)
        trs = []
        for h in range(8):
            if h == k:
                continue
            for n, c in enumerate(sh[h]):
                trs.append(tr(T.xs[c], [(chip * 8 + h, T.H[n])], 1 << len(trs), S.h))
        fused(trs)
        exchange([T.xs[c] for c in sh[k]])
    else:
        g.wait_ge(S.h, len(sh[k]))
        exchange([T.H[n] for n in range(len(sh[k]))])

    def column(s, i):
        col = 256 * chip + 16 * i + (k + 8 * s)
        return T.Y[:, col:col + 1], T.A[:, 16 * s + i:16 * s + i + 1]

    for s in (0, 1):
        need = 16 if k + 8 * s == chip else 4
        q = g.sync if s == 0 else g.scalar
        g.wait_ge(S["a%d" % s], need)
        q.wait_ge(S["a%d" % s], need)
        for i in (2 * k, 2 * k + 1):
            dst, src = column(s, i)
            q.dma_start(dst, src).then_inc(S.b, 16)
    for group in (CAP, NON):
        trs = []
        for w in group:
            if w == k:
                continue
            for s in (0, 1):
                for i in (2 * w, 2 * w + 1):
                    dst, src = column(s, i)
                    trs.append(tr(src, [(chip * 8 + w, dst)], 1 << len(trs), S.b))
        fused(trs)

    B_ALL = 28 + 64
    g.wait_ge(S.b, B_ALL)
    lo = 256 * chip + 32 * k
    mine = T.Y[:, lo:lo + 32]
    fk = fwd_core(chip, k)
    fsem = S["fw%d" % chip]
    dsts = []
    for t in range(1, 8):
        b = (chip + 2 * t) % 16
        dsts.append((b * 8 + fwd_core(b, k), mine))
    trs = [tr(mine, dsts, 0x00FF, fsem)]
    if fk != k:
        trs.append(tr(mine, [(chip * 8 + fk, mine)], 0x0F00, fsem))
    if kr != k:
        trs.append(tr(mine, [(chip * 8 + kr, mine)], 0xF000, S["ry%d" % chip]))
    fused(trs)

    if k in CAP and not is_rank:
        mate = chip ^ 1
        ws = [w for w in range(8) if fwd_core(chip, w) == k]
        for t in range(8):
            c = (chip - 2 * t) % 16
            need = 8 * len(ws) if c != chip else 4 * len([w for w in ws if w != k])
            g.wait_ge(S["fw%d" % c], need)
            lo = 256 * c + 32 * min(ws)
            part = T.Y[:, lo:lo + 32 * len(ws)]
            rsem = S["ry%d" % c]
            trs = [tr(part, [(mate * 8 + mate % 8, part)], 0x00FF, rsem)]
            if c != chip:
                trs.append(tr(part, [(chip * 8 + kr, part)], 0xFF00, rsem))
            fused(trs)

    if is_rank:
        nfw = 8 * (3 if k in CAP else 4)
        for t in range(8):
            c = (chip - 2 * t) % 16
            q = g.sync
            if c == chip:
                q.wait_ge(S.b, B_ALL)
                q.wait_ge(S["ry%d" % c], 28)
            else:
                q.wait_ge(S["ry%d" % c], nfw)
            q.dma_start(T.y[8 * c:8 * c + 8, :], T.Y[:, 256 * c:256 * c + 256]).then_inc(S.st, 16)
        for t in range(8):
            c = ((chip ^ 1) - 2 * t) % 16
            q = g.scalar
            q.wait_ge(S["ry%d" % c], nfw)
            q.dma_start(T.y[8 * c:8 * c + 8, :], T.Y[:, 256 * c:256 * c + 256]).then_inc(S.st, 16)
        g.wait_ge(S.st, 256)

    g.wait_ge(S.snd, sent[0])
